import numpy as np
import ml_dtypes

BF16 = ml_dtypes.bfloat16


def bf(x):
    return np.asarray(x, np.float32).astype(BF16)


def f32(x):
    return np.asarray(x, np.float32)


def f64(x):
    return np.asarray(x).astype(np.float64)


def striped(idx):
    return np.tile(idx.reshape(-1, 16).T, (8, 1))


S, K, M, N, D, V = 512, 128, 512, 256, 4, 64


def setup_inputs():
    return {"table": bf(np.random.standard_normal((K, S))), "w": bf(np.random.standard_normal((K, M)) / np.sqrt(D * K)), "b": f32(0.5 * np.random.standard_normal((M, 1))), "offs": striped(np.random.permutation(S)[:N])}


def reference(table, w, b, offs):
    idx = offs[:16].T.reshape(-1)
    x = f64(table)[:, idx]
    y = f64(w).T @ sum(x[:, t * V : (t + 1) * V] for t in range(D))
    return y + f64(b)

@@ -1,0 +1,48 @@
+import concourse.mybir as mybir
+
+P = 128
+NODES = 512
+M = 512
+LIST = 256
+NEIGHBOURS = 4
+V = LIST // NEIGHBOURS
+PIECE_COLUMNS = V // 16
+M_BLOCKS = M // P
+
+FLOPS = 2 * P * M * V
+
+BF16, F32, U16 = mybir.dt.bfloat16, mybir.dt.float32, mybir.dt.uint16
+ADD = mybir.AluOpType.add
+
+
+def tile_gather_matmul_kernel(tc, table, w, b, offs, out):
+    nc = tc.nc
+    with (
+        tc.tile_pool(name="held", bufs=1) as held,
+        tc.tile_pool(name="results", bufs=M_BLOCKS) as results,
+        tc.psum_pool(name="banks", bufs=M_BLOCKS) as banks,
+    ):
+        offsets = held.tile([P, LIST // 16], U16, name="offsets")
+        nc.sync.dma_start(offsets[:], offs)
+        nodes = held.tile([P, NODES], BF16, name="nodes")
+        nc.scalar.dma_start(nodes[:], table)
+        weights = held.tile([P, M], BF16, name="weights")
+        nc.sync.dma_start(weights[:], w)
+        bias = held.tile([P, M_BLOCKS], F32, name="bias")
+        with nc.allow_non_contiguous_dma(reason="512 single float32 values, one to a partition and block"):
+            nc.gpsimd.dma_start(bias[:], b.rearrange("(a p) o -> p (a o)", p=P))
+
+        for a in range(M_BLOCKS):
+            bank = banks.tile([P, V], F32, name="bank")
+            for t in range(NEIGHBOURS):
+                piece = offsets[:, t * PIECE_COLUMNS : (t + 1) * PIECE_COLUMNS]
+                nc.tensor.matmul(
+                    bank[:],
+                    weights[:, a * P : (a + 1) * P],
+                    nodes[:].indirect(piece),
+                    start=(t == 0),
+                    stop=(t == NEIGHBOURS - 1),
+                )
+            result = results.tile([P, V], F32, name="result")
+            nc.vector.tensor_scalar(result[:], bank[:], bias[:, a : a + 1], None, ADD)
+            nc.sync.dma_start(out[a * P : (a + 1) * P, :], result[:])

@@ -8,6 +8,8 @@ NEIGHBOURS = 4
 V = LIST // NEIGHBOURS
 PIECE_COLUMNS = V // 16
 M_BLOCKS = M // P
+WARM_COLUMNS = 512
+WARM_MATMULS = 3
 
 FLOPS = 2 * P * M * V
 
@@ -21,6 +23,7 @@ def tile_gather_matmul_kernel(tc, table, w, b, offs, out):
         tc.tile_pool(name="held", bufs=1) as held,
         tc.tile_pool(name="results", bufs=M_BLOCKS) as results,
         tc.psum_pool(name="banks", bufs=M_BLOCKS) as banks,
+        tc.psum_pool(name="idle", bufs=1) as idle,
     ):
         offsets = held.tile([P, LIST // 16], U16, name="offsets")
         nc.sync.dma_start(offsets[:], offs)
@@ -30,7 +33,13 @@ def tile_gather_matmul_kernel(tc, table, w, b, offs, out):
         nc.sync.dma_start(weights[:], w)
         bias = held.tile([P, M_BLOCKS], F32, name="bias")
         with nc.allow_non_contiguous_dma(reason="512 single float32 values, one to a partition and block"):
-            nc.gpsimd.dma_start(bias[:], b.rearrange("(a p) o -> p (a o)", p=P))
+            nc.scalar.dma_start(bias[:], b.rearrange("(a p) o -> p (a o)", p=P))
+
+        zeros = held.tile([P, WARM_COLUMNS], BF16, name="zeros")
+        nc.vector.memset(zeros[:], 0.0)
+        unread = idle.tile([P, WARM_COLUMNS], F32, name="unread")
+        for i in range(WARM_MATMULS):
+            nc.tensor.matmul(unread[:], zeros[:, 0:P], zeros[:], start=True, stop=True)
 
         for a in range(M_BLOCKS):
             bank = banks.tile([P, V], F32, name="bank")

@@ -25,12 +25,12 @@ def tile_gather_matmul_kernel(tc, table, w, b, offs, out):
         tc.psum_pool(name="banks", bufs=M_BLOCKS) as banks,
         tc.psum_pool(name="idle", bufs=1) as idle,
     ):
-        offsets = held.tile([P, LIST // 16], U16, name="offsets")
-        nc.sync.dma_start(offsets[:], offs)
-        nodes = held.tile([P, NODES], BF16, name="nodes")
-        nc.scalar.dma_start(nodes[:], table)
         weights = held.tile([P, M], BF16, name="weights")
         nc.sync.dma_start(weights[:], w)
+        nodes = held.tile([P, NODES], BF16, name="nodes")
+        nc.scalar.dma_start(nodes[:], table)
+        offsets = held.tile([P, LIST // 16], U16, name="offsets")
+        nc.sync.dma_start(offsets[:], offs)
         bias = held.tile([P, M_BLOCKS], F32, name="bias")
         with nc.allow_non_contiguous_dma(reason="512 single float32 values, one to a partition and block"):
             nc.scalar.dma_start(bias[:], b.rearrange("(a p) o -> p (a o)", p=P))

@@ -10,6 +10,8 @@ PIECE_COLUMNS = V // 16
 M_BLOCKS = M // P
 WARM_COLUMNS = 512
 WARM_MATMULS = 3
+ROW_ALIGN = 256
+BIAS_STEP = ROW_ALIGN // 4
 
 FLOPS = 2 * P * M * V
 
@@ -25,15 +27,15 @@ def tile_gather_matmul_kernel(tc, table, w, b, offs, out):
         tc.psum_pool(name="banks", bufs=M_BLOCKS) as banks,
         tc.psum_pool(name="idle", bufs=1) as idle,
     ):
-        weights = held.tile([P, M], BF16, name="weights")
+        weights = held.tile([P, M], BF16, name="weights", align_bytes=ROW_ALIGN)
         nc.sync.dma_start(weights[:], w)
-        nodes = held.tile([P, NODES], BF16, name="nodes")
+        nodes = held.tile([P, NODES], BF16, name="nodes", align_bytes=ROW_ALIGN)
         nc.scalar.dma_start(nodes[:], table)
-        offsets = held.tile([P, LIST // 16], U16, name="offsets")
+        offsets = held.tile([P, LIST // 16], U16, name="offsets", align_bytes=ROW_ALIGN)
         nc.sync.dma_start(offsets[:], offs)
-        bias = held.tile([P, M_BLOCKS], F32, name="bias")
+        bias = held.tile([P, M_BLOCKS, BIAS_STEP], F32, name="bias", align_bytes=ROW_ALIGN)
         with nc.allow_non_contiguous_dma(reason="512 single float32 values, one to a partition and block"):
-            nc.scalar.dma_start(bias[:], b.rearrange("(a p) o -> p (a o)", p=P))
+            nc.scalar.dma_start(bias[:, :, 0:1], b.rearrange("(a p) o -> p a o", p=P))
 
         zeros = held.tile([P, WARM_COLUMNS], BF16, name="zeros")
         nc.vector.memset(zeros[:], 0.0)
@@ -52,6 +54,6 @@ def tile_gather_matmul_kernel(tc, table, w, b, offs, out):
                     start=(t == 0),
                     stop=(t == NEIGHBOURS - 1),
                 )
-            result = results.tile([P, V], F32, name="result")
-            nc.vector.tensor_scalar(result[:], bank[:], bias[:, a : a + 1], None, ADD)
+            result = results.tile([P, V], F32, name="result", align_bytes=ROW_ALIGN)
+            nc.vector.tensor_scalar(result[:], bank[:], bias[:, a, 0:1], None, ADD)
             nc.sync.dma_start(out[a * P : (a + 1) * P, :], result[:])

@@ -8,6 +8,8 @@ NEIGHBOURS = 4
 V = LIST // NEIGHBOURS
 PIECE_COLUMNS = V // 16
 M_BLOCKS = M // P
+HALF_BLOCKS = M_BLOCKS // 2
+HALF = HALF_BLOCKS * P
 WARM_COLUMNS = 512
 WARM_MATMULS = 3
 ROW_ALIGN = 256
@@ -27,15 +29,16 @@ def tile_gather_matmul_kernel(tc, table, w, b, offs, out):
         tc.psum_pool(name="banks", bufs=M_BLOCKS) as banks,
         tc.psum_pool(name="idle", bufs=1) as idle,
     ):
-        weights = held.tile([P, M], BF16, name="weights", align_bytes=ROW_ALIGN)
-        nc.sync.dma_start(weights[:], w)
         nodes = held.tile([P, NODES], BF16, name="nodes", align_bytes=ROW_ALIGN)
-        nc.scalar.dma_start(nodes[:], table)
+        nc.sync.dma_start(nodes[:], table)
+        halves = [held.tile([P, HALF], BF16, name=f"half{h}", align_bytes=ROW_ALIGN) for h in range(2)]
+        nc.sync.dma_start(halves[0][:], w[:, 0:HALF])
         offsets = held.tile([P, LIST // 16], U16, name="offsets", align_bytes=ROW_ALIGN)
         nc.sync.dma_start(offsets[:], offs)
+        nc.sync.dma_start(halves[1][:], w[:, HALF:M])
         bias = held.tile([P, M_BLOCKS, BIAS_STEP], F32, name="bias", align_bytes=ROW_ALIGN)
         with nc.allow_non_contiguous_dma(reason="512 single float32 values, one to a partition and block"):
-            nc.scalar.dma_start(bias[:, :, 0:1], b.rearrange("(a p) o -> p a o", p=P))
+            nc.sync.dma_start(bias[:, :, 0:1], b.rearrange("(a p) o -> p a o", p=P))
 
         zeros = held.tile([P, WARM_COLUMNS], BF16, name="zeros")
         nc.vector.memset(zeros[:], 0.0)
@@ -43,17 +46,24 @@ def tile_gather_matmul_kernel(tc, table, w, b, offs, out):
         for i in range(WARM_MATMULS):
             nc.tensor.matmul(unread[:], zeros[:, 0:P], zeros[:], start=True, stop=True)
 
+        first_half = results.tile([P, HALF_BLOCKS, V], F32, name="first_half", align_bytes=ROW_ALIGN)
         for a in range(M_BLOCKS):
             bank = banks.tile([P, V], F32, name="bank")
+            column = a % HALF_BLOCKS * P
             for t in range(NEIGHBOURS):
                 piece = offsets[:, t * PIECE_COLUMNS : (t + 1) * PIECE_COLUMNS]
                 nc.tensor.matmul(
                     bank[:],
-                    weights[:, a * P : (a + 1) * P],
+                    halves[a // HALF_BLOCKS][:, column : column + P],
                     nodes[:].indirect(piece),
                     start=(t == 0),
                     stop=(t == NEIGHBOURS - 1),
                 )
-            result = results.tile([P, V], F32, name="result", align_bytes=ROW_ALIGN)
-            nc.vector.tensor_scalar(result[:], bank[:], bias[:, a, 0:1], None, ADD)
-            nc.sync.dma_start(out[a * P : (a + 1) * P, :], result[:])
+            if a < HALF_BLOCKS:
+                nc.vector.tensor_scalar(first_half[:, a, :], bank[:], bias[:, a, 0:1], None, ADD)
+            else:
+                result = results.tile([P, V], F32, name="result", align_bytes=ROW_ALIGN)
+                nc.vector.tensor_scalar(result[:], bank[:], bias[:, a, 0:1], None, ADD)
+                nc.sync.dma_start(out[a * P : (a + 1) * P, :], result[:])
+            if a == HALF_BLOCKS - 1:
+                nc.sync.dma_start(out[0:HALF, :].rearrange("(a p) v -> p a v", p=P), first_half[:])

@@ -31,11 +31,12 @@ def tile_gather_matmul_kernel(tc, table, w, b, offs, out):
     ):
         nodes = held.tile([P, NODES], BF16, name="nodes", align_bytes=ROW_ALIGN)
         nc.sync.dma_start(nodes[:], table)
-        halves = [held.tile([P, HALF], BF16, name=f"half{h}", align_bytes=ROW_ALIGN) for h in range(2)]
-        nc.sync.dma_start(halves[0][:], w[:, 0:HALF])
+        first_weights = held.tile([P, P], BF16, name="first_weights", align_bytes=ROW_ALIGN)
+        nc.sync.dma_start(first_weights[:], w[:, 0:P])
         offsets = held.tile([P, LIST // 16], U16, name="offsets", align_bytes=ROW_ALIGN)
         nc.sync.dma_start(offsets[:], offs)
-        nc.sync.dma_start(halves[1][:], w[:, HALF:M])
+        later_weights = held.tile([P, M - P], BF16, name="later_weights", align_bytes=ROW_ALIGN)
+        nc.sync.dma_start(later_weights[:], w[:, P:M])
         bias = held.tile([P, M_BLOCKS, BIAS_STEP], F32, name="bias", align_bytes=ROW_ALIGN)
         with nc.allow_non_contiguous_dma(reason="512 single float32 values, one to a partition and block"):
             nc.sync.dma_start(bias[:, :, 0:1], b.rearrange("(a p) o -> p a o", p=P))
@@ -49,12 +50,12 @@ def tile_gather_matmul_kernel(tc, table, w, b, offs, out):
         first_half = results.tile([P, HALF_BLOCKS, V], F32, name="first_half", align_bytes=ROW_ALIGN)
         for a in range(M_BLOCKS):
             bank = banks.tile([P, V], F32, name="bank")
-            column = a % HALF_BLOCKS * P
+            block_weights = first_weights[:] if a == 0 else later_weights[:, (a - 1) * P : a * P]
             for t in range(NEIGHBOURS):
                 piece = offsets[:, t * PIECE_COLUMNS : (t + 1) * PIECE_COLUMNS]
                 nc.tensor.matmul(
                     bank[:],
-                    halves[a // HALF_BLOCKS][:, column : column + P],
+                    block_weights,
                     nodes[:].indirect(piece),
                     start=(t == 0),
                     stop=(t == NEIGHBOURS - 1),

import concourse.mybir as mybir

P = 128
NODES = 512
M = 512
LIST = 256
NEIGHBOURS = 4
V = LIST // NEIGHBOURS
PIECE_COLUMNS = V // 16
M_BLOCKS = M // P
HALF_BLOCKS = M_BLOCKS // 2
HALF = HALF_BLOCKS * P
WARM_COLUMNS = 512
WARM_MATMULS = 3
ROW_ALIGN = 256
BIAS_STEP = ROW_ALIGN // 4

FLOPS = 2 * P * M * V

BF16, F32, U16 = mybir.dt.bfloat16, mybir.dt.float32, mybir.dt.uint16
ADD = mybir.AluOpType.add


def tile_gather_matmul_kernel(tc, table, w, b, offs, out):
    nc = tc.nc
    with (
        tc.tile_pool(name="held", bufs=1) as held,
        tc.tile_pool(name="results", bufs=M_BLOCKS) as results,
        tc.psum_pool(name="banks", bufs=M_BLOCKS) as banks,
        tc.psum_pool(name="idle", bufs=1) as idle,
    ):
        nodes = held.tile([P, NODES], BF16, name="nodes", align_bytes=ROW_ALIGN)
        nc.sync.dma_start(nodes[:], table)
        first_weights = held.tile([P, P], BF16, name="first_weights", align_bytes=ROW_ALIGN)
        nc.sync.dma_start(first_weights[:], w[:, 0:P])
        offsets = held.tile([P, LIST // 16], U16, name="offsets", align_bytes=ROW_ALIGN)
        nc.sync.dma_start(offsets[:], offs)
        later_weights = held.tile([P, M - P], BF16, name="later_weights", align_bytes=ROW_ALIGN)
        nc.sync.dma_start(later_weights[:], w[:, P:M])
        bias = held.tile([P, M_BLOCKS, BIAS_STEP], F32, name="bias", align_bytes=ROW_ALIGN)
        with nc.allow_non_contiguous_dma(reason="512 single float32 values, one to a partition and block"):
            nc.sync.dma_start(bias[:, :, 0:1], b.rearrange("(a p) o -> p a o", p=P))

        zeros = held.tile([P, WARM_COLUMNS], BF16, name="zeros")
        nc.vector.memset(zeros[:], 0.0)
        unread = idle.tile([P, WARM_COLUMNS], F32, name="unread")
        for i in range(WARM_MATMULS):
            nc.tensor.matmul(unread[:], zeros[:, 0:P], zeros[:], start=True, stop=True)

        first_half = results.tile([P, HALF_BLOCKS, V], F32, name="first_half", align_bytes=ROW_ALIGN)
        for a in range(M_BLOCKS):
            bank = banks.tile([P, V], F32, name="bank")
            block_weights = first_weights[:] if a == 0 else later_weights[:, (a - 1) * P : a * P]
            for t in range(NEIGHBOURS):
                piece = offsets[:, t * PIECE_COLUMNS : (t + 1) * PIECE_COLUMNS]
                nc.tensor.matmul(
                    bank[:],
                    block_weights,
                    nodes[:].indirect(piece),
                    start=(t == 0),
                    stop=(t == NEIGHBOURS - 1),
                )
            if a < HALF_BLOCKS:
                nc.vector.tensor_scalar(first_half[:, a, :], bank[:], bias[:, a, 0:1], None, ADD)
            else:
                result = results.tile([P, V], F32, name="result", align_bytes=ROW_ALIGN)
                nc.vector.tensor_scalar(result[:], bank[:], bias[:, a, 0:1], None, ADD)
                nc.sync.dma_start(out[a * P : (a + 1) * P, :], result[:])
            if a == HALF_BLOCKS - 1:
                nc.sync.dma_start(out[0:HALF, :].rearrange("(a p) v -> p a v", p=P), first_half[:])
